import numpy as np
import ml_dtypes


def mxq(x, axis, fmt="e4m3"):
    dtype, down = {"e4m3": (ml_dtypes.float8_e4m3fn, 7), "e5m2": (ml_dtypes.float8_e5m2, 14)}[fmt]
    v = np.moveaxis(np.asarray(x, np.float32).astype(ml_dtypes.bfloat16).astype(np.float64), axis, -1)
    blocks = v.reshape(v.shape[:-1] + (-1, 32))
    amax = np.abs(blocks).max(-1, keepdims=True)
    byte = np.maximum(np.where(amax > 0, np.frexp(amax)[1] - 1 + 127, 0) - down, 1)
    scale = np.exp2(byte - 127.0)
    codes = (blocks / scale).astype(np.float32).astype(dtype).astype(np.float64)
    return np.moveaxis((codes * scale).reshape(v.shape), -1, axis)


WIDE = False


def mx_kscale(k):
    if not WIDE:
        return np.ones(k)
    levels = np.array([10, -10, 5, -5, 0])
    if k % 512:
        return np.exp2(np.random.permutation(np.resize(levels, k // 32))).repeat(32)
    a = np.empty((k // 512, 16))
    for p in range(k // 512):
        a[p, :8] = np.random.permutation(np.resize(levels, 8))
        for g in range(8):
            far = levels[np.abs(levels - a[p, g]) >= 10]
            a[p, g + 8] = far[np.random.randint(len(far))]
    return np.exp2(a.ravel()).repeat(32)


def f64(x):
    return np.asarray(x).astype(np.float64)


def striped(idx):
    return np.tile(idx.reshape(-1, 16).T, (8, 1)).astype(np.uint16)


def unstriped(offs):
    return offs[:16].T.reshape(-1).astype(np.int64)


E2M1 = np.array([0.0, 0.5, 1.0, 1.5, 2.0, 3.0, 4.0, 6.0, -0.0, -0.5, -1.0, -1.5, -2.0, -3.0, -4.0, -6.0])


def pack_weight(w, fmt):
    k, n = w.shape
    w = f64(np.asarray(w, np.float32).astype(ml_dtypes.bfloat16)).reshape(k // 32, 32, n)
    amax = np.abs(w).max(1)
    if fmt == "e4m3":
        byte = np.frexp(amax)[1] - 1 + 127 - 7
    else:
        mant, ex = np.frexp(amax / 6.0)
        byte = np.where(mant > 0.5, ex, ex - 1) + 127
    byte = np.clip(np.where(amax > 0, byte, 1), 1, 254)
    scaled = (w * np.exp2(127.0 - byte)[:, None, :]).reshape(k, n).astype(np.float32)
    by_word = np.ascontiguousarray(scaled.reshape(k // 512, 128, 4, n).transpose(0, 1, 3, 2))
    if fmt == "e4m3":
        words = by_word.astype(ml_dtypes.float8_e4m3fn).view(np.uint8)
    else:
        c = by_word.astype(ml_dtypes.float4_e2m1fn).view(np.uint8) & 0xF
        words = (c[..., 0::2] | (c[..., 1::2] << 4)).reshape(k // 512, 128, 2 * n)
    return np.ascontiguousarray(words), np.ascontiguousarray(byte.astype(np.uint8).reshape(k // 512, 16, n))


def unpack_weight(words, scales, fmt):
    g, _, n = scales.shape
    words = np.ascontiguousarray(words).reshape(g, 128, n, -1)
    if fmt == "e4m3":
        vals = words.view(ml_dtypes.float8_e4m3fn).astype(np.float64)
    else:
        nib = np.empty((g, 128, n, 4), np.uint8)
        nib[..., 0::2] = words & 0xF
        nib[..., 1::2] = words >> 4
        vals = E2M1[nib]
    vals = vals * np.repeat(np.exp2(scales.astype(np.float64) - 127.0), 8, axis=1)[..., None]
    return vals.transpose(0, 1, 3, 2).reshape(g * 512, n)


def gelu(v):
    return 0.5 * v * (1.0 + np.tanh(np.sqrt(2.0 / np.pi) * (v + 0.044715 * v**3)))


K, T, T3, S, T2, P, H, N = 1024, 2048, 1024, 512, 2048, 1024, 1024, 512

def setup_inputs():
    n = np.random.standard_normal
    s = mx_kscale(K)[:, None]
    u = mx_kscale(H)[:, None]
    perm = np.random.permutation(T2)
    d = {}
    d["tab_words"], d["tab_scales"] = pack_weight(n((K, T)) * s, "e4m3")
    d["tab2_words"], d["tab2_scales"] = pack_weight(n((K, T3)) * s, "e4m3")
    d["offs"] = striped(np.random.permutation(T)[:S])
    d["offs2"] = striped(np.random.permutation(T3)[:S])
    d["offs3"] = striped(perm[:S])
    d["offs4"] = striped(perm[S:2 * S])
    d["offs5"] = striped(np.random.permutation(T2)[:P])
    d["w1"] = (1.4 * n((K, H)) / K ** 0.5 / s).astype(np.float32)
    d["w2_words"], d["w2_scales"] = pack_weight(1.8 * n((H, H)) / H ** 0.5 / u, "e2m1")
    d["w3_words"], d["w3_scales"] = pack_weight(0.9 * n((K, H)) / K ** 0.5 / s, "e4m3")
    d["w4"] = (1.5 * n((H, N)) / H ** 0.5 / u).astype(np.float32)
    d["gain1"] = (np.exp(0.3 * n(H)) * u[:, 0]).astype(np.float32)
    d["gain2"] = (np.exp(0.3 * n(H)) * u[:, 0]).astype(np.float32)
    d["page0"] = (0.9 * n((H, T2))).astype(np.float32)
    d["wg1"] = np.exp(0.3 * n((128, S))).astype(np.float32)
    d["wg2"] = np.exp(0.3 * n((128, S))).astype(np.float32)
    return d

def reference(tab_words, tab_scales, tab2_words, tab2_scales, offs, offs2, offs3, offs4, offs5, w1, w2_words, w2_scales, w3_words, w3_scales, w4, gain1, gain2, page0, wg1, wg2):
    v = unpack_weight(tab_words, tab_scales, "e4m3")[:, unstriped(offs)]
    v2 = unpack_weight(tab2_words, tab2_scales, "e4m3")[:, unstriped(offs2)]
    b = mxq(f64(w1), 0, "e4m3").T @ v
    t = np.tanh(b) * f64(gain1)[:, None]
    h1 = b + (unpack_weight(w2_words, w2_scales, "e2m1").T @ mxq(t, 0, "e4m3"))
    h2 = np.square(unpack_weight(w3_words, w3_scales, "e4m3").T @ v2)
    page = f64(page0).copy()
    page[:, unstriped(offs3)] = np.tile(f64(wg1), (H // 128, 1)) * h1
    page[:, unstriped(offs4)] = np.tile(f64(wg2), (H // 128, 1)) * h2
    x = page[:, unstriped(offs5)]
    y = np.tanh(x) * f64(gain2)[:, None]
    return mxq(f64(w4), 0, "e4m3").T @ mxq(y, 0, "e4m3")

@@ -1,0 +1,326 @@
+from contextlib import ExitStack
+
+import concourse.mybir as mybir
+
+K, T, T3, S, T2, PJ, H, N = 1024, 2048, 1024, 512, 2048, 1024, 1024, 512
+FLOPS = 2 * S * K * H * 3 + 2 * PJ * H * N
+
+F32 = mybir.dt.float32
+BF16 = mybir.dt.bfloat16
+I32 = mybir.dt.int32
+U32 = mybir.dt.uint32
+U16 = mybir.dt.uint16
+U8 = mybir.dt.uint8
+FP8X4 = mybir.dt.float8_e4m3fn_x4
+FP4X4 = mybir.dt.float4_e2m1fn_x4
+ACT = mybir.ActivationFunctionType
+MULT = mybir.AluOpType.mult
+ADD = mybir.AluOpType.add
+
+P = 128
+PASS = 512
+SLICES = H // P
+CH = 256
+AL = 64
+
+
+def tile_list_ballot_batch_slots_kernel(
+    tc, tab_words, tab_scales, tab2_words, tab2_scales, offs, offs2, offs3, offs4, offs5,
+    w1, w2_words, w2_scales, w3_words, w3_scales, w4, gain1, gain2, page0, wg1, wg2, out,
+):
+    nc = tc.nc
+    with ExitStack() as ctx:
+        lists = ctx.enter_context(tc.tile_pool(name="lists", bufs=1))
+        sb = ctx.enter_context(tc.tile_pool(name="sb", bufs=1))
+        ring = ctx.enter_context(tc.tile_pool(name="ring", bufs=3))
+        psum = ctx.enter_context(tc.psum_pool(name="psum", bufs=1))
+
+        def tile(shape, dtype, name, tag=None):
+            return sb.tile(shape, dtype, name=name, tag=tag or name, align_bytes=AL)
+
+        def bank(i, name):
+            return psum.tile([P, 512], F32, name=name, tag="bank%d" % i)
+
+        def load_list(src, name):
+            dst = lists.tile(list(src.shape), U16, name=name)
+            nc.sync.dma_start(dst[:], src)
+            return dst
+
+        def load_words(dst, words, a):
+            nc.sync.dma_start(out=dst, in_=words[a].rearrange("p t i -> p (t i)").bitcast(I32))
+
+        def zeroed(shape, name):
+            dst = tile(shape, U8, name)
+            nc.vector.memset(dst[:].bitcast(I32), 0)
+            return dst
+
+        def load_packed_scales(dst, scales):
+            for q in range(4):
+                nc.sync.dma_start(out=dst[32 * q : 32 * q + 8, :].bitcast(I32), in_=scales[:, 4 * q : 4 * q + 4, :].bitcast(I32))
+
+        def load_wg(src, name, tag):
+            dst = tile([P, 4, S], F32, name, tag)
+            for q in (0, 2, 1, 3):
+                nc.sync.dma_start(out=dst[32 * q : 32 * q + 32, :, :], in_=src.rearrange("(p t) s -> p t s", t=4))
+            return dst
+
+        def load_gain(src, name):
+            dst = tile([P, 2, 4], F32, name)
+            nc.sync.dma_start(out=dst[:], in_=src.rearrange("(a p t) -> p a t", a=2, t=4))
+            return dst
+
+        def load_page(s):
+            a, t = divmod(s, 4)
+            dst = tile([P, T2], F32, "page%d" % s)
+            nc.sync.dma_start(out=dst[:], in_=page0[PASS * a : PASS * (a + 1), :].rearrange("(p t) c -> p t c", t=4)[:, t, :])
+            return dst
+
+        def load_rows(src, a, cols, name, tag):
+            dst = tile([P, 4, 512], F32, name, tag)
+            nc.sync.dma_start(out=dst[:], in_=src[PASS * a : PASS * (a + 1), cols].rearrange("(p j) c -> p j c", j=4))
+            return dst
+
+        def quantize(codes, scales, grouped):
+            nc.vector.quantize_mx(out=codes.bitcast(FP8X4), scales=scales, in_=grouped)
+
+        def interleave(copy, rows, width, name):
+            grouped = ring.tile([P, 4 * width], BF16, name=name, tag="grouped", align_bytes=AL)
+            copy(out=grouped[:].rearrange("p (c i t) -> p c t i", i=4, t=4), in_=rows.rearrange("p t (c i) -> p c t i", i=4))
+            return grouped
+
+        tab2_sc = zeroed([P, T3], "tab2_sc")
+        tab_sc = zeroed([P, T], "tab_sc")
+        w3_sc_raw = zeroed([P, H], "w3_sc_raw")
+        w2_sc_raw = zeroed([P, 2 * H], "w2_sc_raw")
+
+        def gather_table(windows, scales, idx, name):
+            codes = [tile([P, S], U32, "%s_%d" % (name, a)) for a in range(2)]
+            for a in range(2):
+                nc.vector.tensor_copy(codes[a][:], windows[a].bitcast(U32).indirect(idx[:]))
+            plane = tile([P, S], U8, name + "_sc")
+            nc.vector.tensor_copy(plane[:], scales[:].indirect(idx[:]))
+            return codes, plane
+
+        idx2 = load_list(offs2, "idx2")
+        idx1 = load_list(offs, "idx1")
+        idx4 = load_list(offs4, "idx4")
+        idx3 = load_list(offs3, "idx3")
+
+        w1_codes = tile([P, 2 * H], U32, "w1_codes", "slotI")
+        w1_sc = tile([P, 2 * H], U8, "w1_sc")
+        b_sb = [tile([P, S], F32, "b_%d" % s) for s in range(SLICES)]
+        t_codes = tile([P, 2 * S], U32, "t_codes")
+        t_sc = tile([P, 2 * S], U8, "t_sc")
+
+        def w1_chunk(a, b):
+            raw = load_rows(w1, a, slice(512 * b, 512 * (b + 1)), "w1_raw%d%d" % (a, b), "slot" + "EFCD"[2 * b + a])
+            grouped = ring.tile([P, 2048], BF16, name="w1_g%d%d" % (a, b), tag="grouped", align_bytes=AL)
+            cast = nc.vector.tensor_copy if b == 0 else nc.scalar.copy
+            cast(out=grouped[:].rearrange("p (t m j) -> p m j t", t=4, j=4), in_=raw[:].rearrange("p j (m t) -> p m j t", t=4))
+            cols = slice(a * H + 512 * b, a * H + 512 * (b + 1))
+            quantize(w1_codes[:, cols], w1_sc[:, cols], grouped[:])
+
+        def first_stage(b):
+            accs = []
+            t_rows = tile([P, 4, S], BF16, "t_rows%d" % b)
+            for t in range(4):
+                s = 4 * b + t
+                acc = bank(s, "b_acc%d" % s)
+                for a in range(2):
+                    cols = slice(a * H + s * P, a * H + (s + 1) * P)
+                    nc.tensor.matmul_mx(
+                        out=acc[:], lhsT=w1_codes[:, cols].bitcast(FP8X4), lhsT_scale=w1_sc[:, cols],
+                        rhs=v[a][:].bitcast(FP8X4), rhs_scale=v_sc[4 * a : P, :], start=(a == 0), stop=(a == 1),
+                    )
+                th = ring.tile([P, S], F32, name="tanh_b%d" % s, tag="tanh_b")
+                nc.scalar.activation(th[:], acc[:], ACT.Tanh)
+                nc.scalar.activation(t_rows[:, t, :], th[:], ACT.Copy, scale=gain1_sb[:, b, t : t + 1])
+                accs.append(acc)
+            grouped = interleave(nc.scalar.copy, t_rows[:], S, "t_g%d" % b)
+            quantize(t_codes[:, b * S : (b + 1) * S], t_sc[:, b * S : (b + 1) * S], grouped[:])
+            for t in range(4):
+                nc.scalar.copy(out=b_sb[4 * b + t][:], in_=accs[t][:])
+
+        h2 = {}
+
+        def square_stage(b):
+            for s in range(4 * b, 4 * b + 4):
+                acc = bank((s + 4) % SLICES, "h2_acc%d" % s)
+                for a in range(2):
+                    nc.tensor.matmul_mx(
+                        out=acc[:], lhsT=w3_d[:, a * H + s * P : a * H + (s + 1) * P].bitcast(FP8X4),
+                        lhsT_scale=w3_sc[4 * a : P, s * P : (s + 1) * P],
+                        rhs=v2[a][:].bitcast(FP8X4), rhs_scale=v2_sc[4 * a : P, :], start=(a == 0), stop=(a == 1),
+                    )
+                h2[s] = tile([P, S], F32, "h2_%d" % s, "h%d" % s)
+                nc.scalar.activation(h2[s][:], acc[:], ACT.Square)
+
+        pages = []
+
+        def next_page():
+            s = len(pages)
+            pages.append(load_page(s))
+            nc.vector.tensor_tensor(pages[s][:].indirect(idx4[:]), h2[s][:], wg2_sb[:, s % 4, :], MULT)
+
+        tab2_w = tile([P, 2 * T3], I32, "tab2_w", "slotA")
+        for a in range(2):
+            load_words(tab2_w[:, a * T3 : (a + 1) * T3], tab2_words, a)
+        load_packed_scales(tab2_sc, tab2_scales)
+        v2, v2_sc = gather_table([tab2_w[:, a * T3 : (a + 1) * T3] for a in range(2)], tab2_sc, idx2, "v2")
+
+        tab_w = [tile([P, T], I32, "tab_w%d" % a, "slot" + "CD"[a]) for a in range(2)]
+        for a in range(2):
+            load_words(tab_w[a][:], tab_words, a)
+        load_packed_scales(tab_sc, tab_scales)
+        v, v_sc = gather_table([w[:] for w in tab_w], tab_sc, idx1, "v")
+
+        w3_raw = tile([P, 2 * H], I32, "w3_raw", "slotB")
+        for a in range(2):
+            load_words(w3_raw[:, a * H : (a + 1) * H], w3_words, a)
+        load_packed_scales(w3_sc_raw, w3_scales)
+        w3_d = tile([P, 2 * H], I32, "w3_d", "slotG")
+        for a in range(2):
+            cols = slice(a * H, (a + 1) * H)
+            nc.vector.tensor_copy(
+                out=w3_d[:, cols].rearrange("p (b t u i) -> p b u t i", b=2, t=4, i=4),
+                in_=w3_raw[:, cols].rearrange("p (b u i t) -> p b u t i", b=2, t=4, i=4),
+            )
+        w3_sc = tile([P, H], U8, "w3_sc")
+        nc.vector.tensor_copy(
+            out=w3_sc[:].rearrange("p (b t q) -> p b t q", b=2, t=4),
+            in_=w3_sc_raw[:].rearrange("p (b q t) -> p b t q", b=2, t=4),
+        )
+
+        square_stage(0)
+        square_stage(1)
+        w2_raw = tile([P, H], I32, "w2_raw", "slotH")
+        nc.sync.dma_start(out=w2_raw[:].rearrange("p (a c) -> p a c", a=2), in_=w2_words.rearrange("a p c -> p a c").bitcast(I32))
+        for q in range(4):
+            nc.sync.dma_start(
+                out=w2_sc_raw[32 * q : 32 * q + 4, :].bitcast(I32).rearrange("r (a c) -> r a c", a=2),
+                in_=w2_scales[:, 4 * q : 4 * q + 4, :].rearrange("a r c -> r a c").bitcast(I32),
+            )
+        w2_d = tile([P, 4 * H], U8, "w2_d")
+        nc.vector.tensor_copy(
+            out=w2_d[:].bitcast(U16).rearrange("p (g t q) -> p g t q", g=4, t=4),
+            in_=w2_raw[:].bitcast(U16).rearrange("p (g q t) -> p g t q", g=4, t=4),
+        )
+        w2_sc = tile([P, 2 * H], U8, "w2_sc")
+        nc.vector.tensor_copy(
+            out=w2_sc[:].rearrange("p (g t q) -> p g t q", g=4, t=4),
+            in_=w2_sc_raw[:].rearrange("p (g q t) -> p g t q", g=4, t=4),
+        )
+
+        w1_chunk(0, 0)
+        gain1_sb = load_gain(gain1, "gain1_sb")
+        w1_chunk(1, 0)
+        first_stage(0)
+        wg2_sb = load_wg(wg2, "wg2_sb", "wg2_sb")
+        next_page()
+        next_page()
+        w1_chunk(0, 1)
+        next_page()
+        w1_chunk(1, 1)
+        first_stage(1)
+        next_page()
+        next_page()
+        wg1_sb = load_wg(wg1, "wg1_sb", "slotG")
+        next_page()
+        next_page()
+        next_page()
+        idx5 = load_list(offs5, "idx5")
+        gain2_sb = load_gain(gain2, "gain2_sb")
+
+        s_acc = []
+        for s in range(SLICES):
+            acc = bank(s, "s_acc%d" % s)
+            for a in range(2):
+                c0 = a * H + s * P
+                nc.tensor.matmul_mx(
+                    out=acc[:], lhsT=w2_d[:, 2 * c0 : 2 * (c0 + P)].bitcast(FP4X4), lhsT_scale=w2_sc[:, c0 : c0 + P],
+                    rhs=t_codes[:, a * S : (a + 1) * S].bitcast(FP8X4), rhs_scale=t_sc[:, a * S : (a + 1) * S],
+                    start=(a == 0), stop=(a == 1),
+                )
+            s_acc.append(acc)
+
+        h1 = {}
+
+        def add_b(s):
+            h1[s] = tile([P, S], F32, "h1_%d" % s, "h%d" % s if s < 2 else "page%d" % (s - 2 + s // (SLICES - 1)))
+            nc.vector.tensor_tensor(h1[s][:], s_acc[s][:], b_sb[s][:], ADD)
+
+        w4_codes = tile([P, 2 * N], U32, "w4_codes", "slotH")
+        w4_sc = tile([P, 2 * N], U8, "w4_sc")
+
+        def w4_pass(a):
+            raw = load_rows(w4, a, slice(0, N), "w4_raw%d" % a, "slot" + "CD"[a])
+            grouped = interleave(nc.scalar.copy, raw[:], N, "w4_g%d" % a)
+            quantize(w4_codes[:, a * N : (a + 1) * N], w4_sc[:, a * N : (a + 1) * N], grouped[:])
+
+        x_sb = tile([P, 2, PJ], F32, "x_sb", "slotE")
+        tanh_x = tile([P, PJ], F32, "tanh_x", "slotF")
+        y_rows = [tile([P, 4, PJ], BF16, "y_rows%d" % a, "slot" + "AB"[a]) for a in range(2)]
+        y_codes = tile([P, 2 * PJ], U32, "y_codes", "slotI")
+        y_sc = tile([P, 2 * PJ], U8, "y_sc")
+
+        def scatter1(s):
+            nc.vector.tensor_tensor(pages[s][:].indirect(idx3[:]), h1[s][:], wg1_sb[:, s % 4, :], MULT)
+
+        def fetch(s, j0, width):
+            a, t = divmod(s, 4)
+            x = x_sb[:, t % 2, j0 : j0 + width]
+            th = tanh_x[:, j0 : j0 + width]
+            nc.vector.tensor_copy(x, pages[s][:].indirect(idx5[:, j0 // 16 : (j0 + width) // 16]))
+            nc.scalar.activation(th, x, ACT.Tanh)
+            nc.scalar.activation(y_rows[a][:, t, j0 : j0 + width], th, ACT.Copy, scale=gain2_sb[:, a, t : t + 1])
+
+        def quantize_y(copy, a, j0, width):
+            grouped = interleave(copy, y_rows[a][:, :, j0 : j0 + width], width, "y_g%d_%d" % (a, j0))
+            cols = slice(a * PJ + j0, a * PJ + j0 + width)
+            quantize(y_codes[:, cols], y_sc[:, cols], grouped[:])
+
+        out_acc = {}
+
+        def out_pass(a, q):
+            cols = slice(a * PJ + q * CH, a * PJ + (q + 1) * CH)
+            for h in range(2):
+                if a == 0:
+                    out_acc[q, h] = bank(2 * q + h, "out_acc%d%d" % (q, h))
+                for e in range(2):
+                    wc = slice(a * N + (2 * h + e) * P, a * N + (2 * h + e + 1) * P)
+                    nc.tensor.matmul_mx(
+                        out=out_acc[q, h][:, e * CH : (e + 1) * CH], lhsT=w4_codes[:, wc].bitcast(FP8X4), lhsT_scale=w4_sc[:, wc],
+                        rhs=y_codes[:, cols].bitcast(FP8X4), rhs_scale=y_sc[:, cols],
+                        start=(a == 0 and e == 0), stop=(a == 1 and e == 1),
+                    )
+
+        add_b(0)
+        add_b(1)
+        for s in range(SLICES - 1):
+            scatter1(s)
+            fetch(s, 0, PJ)
+            if s + 2 < SLICES - 1:
+                add_b(s + 2)
+            if s < 2:
+                w4_pass(s)
+            if s in (3, 4):
+                quantize_y(nc.scalar.copy, 0, (s - 3) * 512, 512)
+        last = SLICES - 1
+        add_b(last)
+        for q in range(PJ // CH):
+            out_pass(0, q)
+        scatter1(last)
+        staged = [tile([P, 4, 2 * CH], F32, "staged%d" % h, "slot" + "CD"[h]) for h in range(2)]
+        out_view = out.rearrange("(c p) j -> p c j", p=P)
+        for q in range(PJ // CH):
+            fetch(last, q * CH, CH)
+        for q in range(PJ // CH):
+            quantize_y(nc.vector.tensor_copy, 1, q * CH, CH)
+            out_pass(1, q)
+            for h in range(2):
+                copy = nc.scalar.copy if (h == 0 or q < 2) else nc.vector.tensor_copy
+                copy(out=staged[h][:, q, :], in_=out_acc[q, h][:])
+                nc.sync.dma_start(
+                    out=out_view[:, 2 * h : 2 * h + 2, q * CH : (q + 1) * CH],
+                    in_=staged[h][:, q, :].rearrange("p (e j) -> p e j", e=2),
+                )

@@ -1,6 +1,7 @@
 from contextlib import ExitStack
 
 import concourse.mybir as mybir
+from concourse.masks import make_identity
 
 K, T, T3, S, T2, PJ, H, N = 1024, 2048, 1024, 512, 2048, 1024, 1024, 512
 FLOPS = 2 * S * K * H * 3 + 2 * PJ * H * N
@@ -58,10 +59,26 @@ def tile_list_ballot_batch_slots_kernel(
             for q in range(4):
                 nc.sync.dma_start(out=dst[32 * q : 32 * q + 8, :].bitcast(I32), in_=scales[:, 4 * q : 4 * q + 4, :].bitcast(I32))
 
-        def load_wg(src, name, tag):
+        def load_wg_dealt(src, name, tag):
             dst = tile([P, 4, S], F32, name, tag)
             for q in (0, 2, 1, 3):
                 nc.sync.dma_start(out=dst[32 * q : 32 * q + 32, :, :], in_=src.rearrange("(p t) s -> p t s", t=4))
+            return dst
+
+        def load_wg(src, name, spare):
+            rows = ring.tile([P, S], F32, name=name + "_rows", tag="tanh_b")
+            nc.sync.dma_start(out=rows[:], in_=src)
+            turned = bank(0, name + "_turned")
+            for c in range(4):
+                nc.tensor.transpose(turned[:, c * P : (c + 1) * P], rows[:, c * P : (c + 1) * P], ident[:])
+            spread = tile([P, 4, 4, 4, 32], F32, name + "_spread", spare)
+            nc.scalar.copy(out=spread[:], in_=turned[:].rearrange("j (c q t) -> j c t q", c=4, t=4).unsqueeze(3).to_broadcast([P, 4, 4, 4, 32]))
+            dst = tile([P, 4, S], F32, name)
+            for t in range(4):
+                back = bank(t, name + "_back%d" % t)
+                for c in range(4):
+                    nc.tensor.transpose(back[:, c * P : (c + 1) * P], spread[:, c, t, :, :].rearrange("j x q -> j (x q)"), ident[:])
+                nc.scalar.copy(out=dst[:, t, :], in_=back[:])
             return dst
 
         def load_gain(src, name):
@@ -83,10 +100,16 @@ def tile_list_ballot_batch_slots_kernel(
         def quantize(codes, scales, grouped):
             nc.vector.quantize_mx(out=codes.bitcast(FP8X4), scales=scales, in_=grouped)
 
-        def interleave(copy, rows, width, name):
-            grouped = ring.tile([P, 4 * width], BF16, name=name, tag="grouped", align_bytes=AL)
+        def interleave(copy, rows, width, name, tag=None):
+            if tag:
+                grouped = tile([P, 4 * width], BF16, name, tag)
+            else:
+                grouped = ring.tile([P, 4 * width], BF16, name=name, tag="grouped", align_bytes=AL)
             copy(out=grouped[:].rearrange("p (c i t) -> p c t i", i=4, t=4), in_=rows.rearrange("p t (c i) -> p c t i", i=4))
             return grouped
+
+        ident = tile([P, P], F32, "ident")
+        make_identity(nc, ident[:])
 
         tab2_sc = zeroed([P, T3], "tab2_sc")
         tab_sc = zeroed([P, T], "tab_sc")
@@ -106,19 +129,26 @@ def tile_list_ballot_batch_slots_kernel(
         idx4 = load_list(offs4, "idx4")
         idx3 = load_list(offs3, "idx3")
 
-        w1_codes = tile([P, 2 * H], U32, "w1_codes", "slotI")
+        w1_codes = {}
+        w1_grouped = {}
         w1_sc = tile([P, 2 * H], U8, "w1_sc")
-        b_sb = [tile([P, S], F32, "b_%d" % s) for s in range(SLICES)]
-        t_codes = tile([P, 2 * S], U32, "t_codes")
+        b_sb = {}
+        b_acc = {}
+        t_codes = {}
         t_sc = tile([P, 2 * S], U8, "t_sc")
 
         def w1_chunk(a, b):
-            raw = load_rows(w1, a, slice(512 * b, 512 * (b + 1)), "w1_raw%d%d" % (a, b), "slot" + "EFCD"[2 * b + a])
+            raw = load_rows(w1, a, slice(512 * b, 512 * (b + 1)), "w1_raw%d%d" % (a, b), "slot" + "EFAB"[2 * b + a])
             grouped = ring.tile([P, 2048], BF16, name="w1_g%d%d" % (a, b), tag="grouped", align_bytes=AL)
             cast = nc.vector.tensor_copy if b == 0 else nc.scalar.copy
             cast(out=grouped[:].rearrange("p (t m j) -> p m j t", t=4, j=4), in_=raw[:].rearrange("p j (m t) -> p m j t", t=4))
+            w1_grouped[a, b] = grouped
+
+        def quantize_w1(a, b):
+            grouped = w1_grouped[a, b]
             cols = slice(a * H + 512 * b, a * H + 512 * (b + 1))
-            quantize(w1_codes[:, cols], w1_sc[:, cols], grouped[:])
+            w1_codes[a, b] = tile([P, 512], U32, "w1_codes%d%d" % (a, b), "h%d" % (3, 4)[a] if b else "slot" + "IH"[a])
+            quantize(w1_codes[a, b][:], w1_sc[:, cols], grouped[:])
 
         def first_stage(b):
             accs = []
@@ -129,7 +159,7 @@ def tile_list_ballot_batch_slots_kernel(
                 for a in range(2):
                     cols = slice(a * H + s * P, a * H + (s + 1) * P)
                     nc.tensor.matmul_mx(
-                        out=acc[:], lhsT=w1_codes[:, cols].bitcast(FP8X4), lhsT_scale=w1_sc[:, cols],
+                        out=acc[:], lhsT=w1_codes[a, b][:, t * P : (t + 1) * P].bitcast(FP8X4), lhsT_scale=w1_sc[:, cols],
                         rhs=v[a][:].bitcast(FP8X4), rhs_scale=v_sc[4 * a : P, :], start=(a == 0), stop=(a == 1),
                     )
                 th = ring.tile([P, S], F32, name="tanh_b%d" % s, tag="tanh_b")
@@ -137,11 +167,20 @@ def tile_list_ballot_batch_slots_kernel(
                 nc.scalar.activation(t_rows[:, t, :], th[:], ACT.Copy, scale=gain1_sb[:, b, t : t + 1])
                 accs.append(acc)
             grouped = interleave(nc.scalar.copy, t_rows[:], S, "t_g%d" % b)
-            quantize(t_codes[:, b * S : (b + 1) * S], t_sc[:, b * S : (b + 1) * S], grouped[:])
+            t_grouped[b] = grouped
+            b_acc[b] = accs
+
+        def keep_b(b):
+            b_sb[b] = tile([P, 4, S], F32, "b_sb%d" % b, ("slotB", "t_rows1")[b])
             for t in range(4):
-                nc.scalar.copy(out=b_sb[4 * b + t][:], in_=accs[t][:])
+                nc.scalar.copy(out=b_sb[b][:, t, :], in_=b_acc[b][t][:])
+
+        def quantize_t(b):
+            t_codes[b] = tile([P, S], U32, "t_codes%d" % b, "h%d" % (2, 7)[b])
+            quantize(t_codes[b][:], t_sc[:, b * S : (b + 1) * S], t_grouped[b][:])
 
         h2 = {}
+        t_grouped = {}
 
         def square_stage(b):
             for s in range(4 * b, 4 * b + 4):
@@ -168,12 +207,7 @@ def tile_list_ballot_batch_slots_kernel(
         load_packed_scales(tab2_sc, tab2_scales)
         v2, v2_sc = gather_table([tab2_w[:, a * T3 : (a + 1) * T3] for a in range(2)], tab2_sc, idx2, "v2")
 
-        tab_w = [tile([P, T], I32, "tab_w%d" % a, "slot" + "CD"[a]) for a in range(2)]
-        for a in range(2):
-            load_words(tab_w[a][:], tab_words, a)
-        load_packed_scales(tab_sc, tab_scales)
-        v, v_sc = gather_table([w[:] for w in tab_w], tab_sc, idx1, "v")
-
+        wg2_sb = load_wg(wg2, "wg2_sb", "page6")
         w3_raw = tile([P, 2 * H], I32, "w3_raw", "slotB")
         for a in range(2):
             load_words(w3_raw[:, a * H : (a + 1) * H], w3_words, a)
@@ -211,23 +245,36 @@ def tile_list_ballot_batch_slots_kernel(
             in_=w2_sc_raw[:].rearrange("p (g q t) -> p g t q", g=4, t=4),
         )
 
+        next_page()
         w1_chunk(0, 0)
+        tab_w = [tile([P, T], I32, "tab_w%d" % a, "slot" + "CD"[a]) for a in range(2)]
+        for a in range(2):
+            load_words(tab_w[a][:], tab_words, a)
+        load_packed_scales(tab_sc, tab_scales)
+        v, v_sc = gather_table([w[:] for w in tab_w], tab_sc, idx1, "v")
+
+        quantize_w1(0, 0)
         gain1_sb = load_gain(gain1, "gain1_sb")
         w1_chunk(1, 0)
-        first_stage(0)
-        wg2_sb = load_wg(wg2, "wg2_sb", "wg2_sb")
         next_page()
+        quantize_w1(1, 0)
+        first_stage(0)
         next_page()
         w1_chunk(0, 1)
         next_page()
         w1_chunk(1, 1)
+        quantize_t(0)
+        quantize_w1(0, 1)
+        next_page()
+        quantize_w1(1, 1)
+        keep_b(0)
         first_stage(1)
-        next_page()
-        next_page()
-        wg1_sb = load_wg(wg1, "wg1_sb", "slotG")
+        keep_b(1)
         next_page()
         next_page()
         next_page()
+        quantize_t(1)
+        wg1_sb = load_wg_dealt(wg1, "wg1_sb", "slotG")
         idx5 = load_list(offs5, "idx5")
         gain2_sb = load_gain(gain2, "gain2_sb")
 
@@ -238,16 +285,32 @@ def tile_list_ballot_batch_slots_kernel(
                 c0 = a * H + s * P
                 nc.tensor.matmul_mx(
                     out=acc[:], lhsT=w2_d[:, 2 * c0 : 2 * (c0 + P)].bitcast(FP4X4), lhsT_scale=w2_sc[:, c0 : c0 + P],
-                    rhs=t_codes[:, a * S : (a + 1) * S].bitcast(FP8X4), rhs_scale=t_sc[:, a * S : (a + 1) * S],
+                    rhs=t_codes[a][:].bitcast(FP8X4), rhs_scale=t_sc[:, a * S : (a + 1) * S],
                     start=(a == 0), stop=(a == 1),
                 )
             s_acc.append(acc)
 
+        s_sb = {}
+        for s, home in zip((2, 3, 4, 5, 7), (1, 5, 3, 4, 2)):
+            s_sb[s] = tile([P, S], F32, "s_sb%d" % s, "h%d" % home)
+            nc.scalar.copy(out=s_sb[s][:], in_=s_acc[s][:])
+
         h1 = {}
 
+        spare = {}
+
         def add_b(s):
-            h1[s] = tile([P, S], F32, "h1_%d" % s, "h%d" % s if s < 2 else "page%d" % (s - 2 + s // (SLICES - 1)))
-            nc.vector.tensor_tensor(h1[s][:], s_acc[s][:], b_sb[s][:], ADD)
+            b = b_sb[s // 4][:, s % 4, :]
+            if s in (0, 1, 6):
+                h1[s] = tile([P, S], F32, "h1_%d" % s, {0: "h6", 1: "h0", 6: "y_half1"}[s])[:]
+                nc.vector.tensor_tensor(h1[s], s_acc[s][:], b, ADD)
+            elif s == 7:
+                h1[s] = tile([P, S], F32, "h1_%d" % s, "y_half1")[:]
+                nc.gpsimd.tensor_tensor(h1[s], s_sb[s][:], b, ADD)
+            else:
+                spare[s - 2] = tile([P, S + PJ], F32, "spare%d" % (s - 2), "page%d" % (s - 2))
+                h1[s] = spare[s - 2][:, :S]
+                nc.gpsimd.tensor_tensor(h1[s], s_sb[s][:], b, ADD)
 
         w4_codes = tile([P, 2 * N], U32, "w4_codes", "slotH")
         w4_sc = tile([P, 2 * N], U8, "w4_sc")
@@ -258,26 +321,33 @@ def tile_list_ballot_batch_slots_kernel(
             quantize(w4_codes[:, a * N : (a + 1) * N], w4_sc[:, a * N : (a + 1) * N], grouped[:])
 
         x_sb = tile([P, 2, PJ], F32, "x_sb", "slotE")
-        tanh_x = tile([P, PJ], F32, "tanh_x", "slotF")
-        y_rows = [tile([P, 4, PJ], BF16, "y_rows%d" % a, "slot" + "AB"[a]) for a in range(2)]
+        x_more = tile([P, 2, PJ], F32, "x_more", "slotF")
+        tanh_x = x_more[:, 0, :]
+        x_home = {0: x_sb[:, 0, :], 1: x_sb[:, 1, :], 2: x_more[:, 1, :]}
+        y_rows = tile([P, 4, PJ], BF16, "y_rows", "slotA")
+        y_woven = tile([P, PJ, 4], BF16, "y_woven", "slotB")
         y_codes = tile([P, 2 * PJ], U32, "y_codes", "slotI")
         y_sc = tile([P, 2 * PJ], U8, "y_sc")
 
         def scatter1(s):
-            nc.vector.tensor_tensor(pages[s][:].indirect(idx3[:]), h1[s][:], wg1_sb[:, s % 4, :], MULT)
+            nc.vector.tensor_tensor(pages[s][:].indirect(idx3[:]), h1[s], wg1_sb[:, s % 4, :], MULT)
 
         def fetch(s, j0, width):
             a, t = divmod(s, 4)
-            x = x_sb[:, t % 2, j0 : j0 + width]
+            x = x_home[s][:, j0 : j0 + width]
             th = tanh_x[:, j0 : j0 + width]
             nc.vector.tensor_copy(x, pages[s][:].indirect(idx5[:, j0 // 16 : (j0 + width) // 16]))
             nc.scalar.activation(th, x, ACT.Tanh)
-            nc.scalar.activation(y_rows[a][:, t, j0 : j0 + width], th, ACT.Copy, scale=gain2_sb[:, a, t : t + 1])
+            gain = gain2_sb[:, a, t : t + 1]
+            if s == SLICES - 1:
+                nc.vector.tensor_scalar(y_woven[:, j0 : j0 + width, t], th, gain, None, MULT)
+            else:
+                y = y_rows[:, t, j0 : j0 + width] if a == 0 else y_woven[:, j0 : j0 + width, t]
+                nc.scalar.activation(y, th, ACT.Copy, scale=gain)
 
-        def quantize_y(copy, a, j0, width):
-            grouped = interleave(copy, y_rows[a][:, :, j0 : j0 + width], width, "y_g%d_%d" % (a, j0))
+        def quantize_y(a, j0, width, grouped):
             cols = slice(a * PJ + j0, a * PJ + j0 + width)
-            quantize(y_codes[:, cols], y_sc[:, cols], grouped[:])
+            quantize(y_codes[:, cols], y_sc[:, cols], grouped)
 
         out_acc = {}
 
@@ -296,26 +366,32 @@ def tile_list_ballot_batch_slots_kernel(
 
         add_b(0)
         add_b(1)
-        for s in range(SLICES - 1):
+        last = SLICES - 1
+        for s in range(SLICES):
+            if 3 <= s < last:
+                x_home[s] = spare[s - 3][:, S:]
+            elif s == last:
+                x_home[s] = tile([P, PJ], F32, "x_last", "page4")[:]
+            if s >= 6:
+                add_b(s)
             scatter1(s)
-            fetch(s, 0, PJ)
-            if s + 2 < SLICES - 1:
+            if s < last:
+                fetch(s, 0, PJ)
+            if s + 2 < 6:
                 add_b(s + 2)
             if s < 2:
                 w4_pass(s)
-            if s in (3, 4):
-                quantize_y(nc.scalar.copy, 0, (s - 3) * 512, 512)
-        last = SLICES - 1
-        add_b(last)
+            if s == 3:
+                for j0 in (0, 512):
+                    quantize_y(0, j0, 512, interleave(nc.scalar.copy, y_rows[:, :, j0 : j0 + 512], 512, "y_g%d" % j0, "y_half%d" % (j0 // 512))[:])
         for q in range(PJ // CH):
             out_pass(0, q)
-        scatter1(last)
         staged = [tile([P, 4, 2 * CH], F32, "staged%d" % h, "slot" + "CD"[h]) for h in range(2)]
         out_view = out.rearrange("(c p) j -> p c j", p=P)
         for q in range(PJ // CH):
             fetch(last, q * CH, CH)
         for q in range(PJ // CH):
-            quantize_y(nc.vector.tensor_copy, 1, q * CH, CH)
+            quantize_y(1, q * CH, CH, y_woven[:, q * CH : (q + 1) * CH, :].rearrange("p j t -> p (j t)"))
             out_pass(1, q)
             for h in range(2):
                 copy = nc.scalar.copy if (h == 0 or q < 2) else nc.vector.tensor_copy

@@ -140,14 +140,14 @@ def tile_list_ballot_batch_slots_kernel(
         def w1_chunk(a, b):
             raw = load_rows(w1, a, slice(512 * b, 512 * (b + 1)), "w1_raw%d%d" % (a, b), "slot" + "EFAB"[2 * b + a])
             grouped = ring.tile([P, 2048], BF16, name="w1_g%d%d" % (a, b), tag="grouped", align_bytes=AL)
-            cast = nc.vector.tensor_copy if b == 0 else nc.scalar.copy
+            cast = nc.vector.tensor_copy if (a, b) == (1, 0) else nc.scalar.copy
             cast(out=grouped[:].rearrange("p (t m j) -> p m j t", t=4, j=4), in_=raw[:].rearrange("p j (m t) -> p m j t", t=4))
             w1_grouped[a, b] = grouped
 
         def quantize_w1(a, b):
             grouped = w1_grouped[a, b]
             cols = slice(a * H + 512 * b, a * H + 512 * (b + 1))
-            w1_codes[a, b] = tile([P, 512], U32, "w1_codes%d%d" % (a, b), "h%d" % (3, 4)[a] if b else "slot" + "IH"[a])
+            w1_codes[a, b] = tile([P, 512], U32, "w1_codes%d%d" % (a, b), "h%d" % (3, 4)[a] if b else "slot" + "DH"[a])
             quantize(w1_codes[a, b][:], w1_sc[:, cols], grouped[:])
 
         def first_stage(b):
@@ -290,27 +290,31 @@ def tile_list_ballot_batch_slots_kernel(
                 )
             s_acc.append(acc)
 
-        s_sb = {}
-        for s, home in zip((2, 3, 4, 5, 7), (1, 5, 3, 4, 2)):
-            s_sb[s] = tile([P, S], F32, "s_sb%d" % s, "h%d" % home)
-            nc.scalar.copy(out=s_sb[s][:], in_=s_acc[s][:])
+        def turn(dst, parts):
+            for c in range(4):
+                cols = slice(c * P, (c + 1) * P)
+                for i, part in enumerate(parts):
+                    nc.tensor.matmul(dst[:, cols], part[:, cols], ident[:], start=(i == 0), stop=(i == len(parts) - 1), is_transpose=True)
+
+        h1_acc = {}
+        for s in (2, 3, 4, 5, 6):
+            s_sb = ring.tile([P, S], F32, name="s_sb%d" % s, tag="tanh_b")
+            nc.scalar.copy(out=s_sb[:], in_=s_acc[s][:])
+            turned = bank(s, "h1_turned%d" % s)
+            turn(turned, [b_sb[s // 4][:, s % 4, :], s_sb])
+            turned_sb = ring.tile([P, S], F32, name="h1_turned_sb%d" % s, tag="tanh_b")
+            nc.scalar.copy(out=turned_sb[:], in_=turned[:])
+            h1_acc[s] = bank(s, "h1_acc%d" % s)
+            turn(h1_acc[s], [turned_sb])
 
         h1 = {}
 
-        spare = {}
-
         def add_b(s):
-            b = b_sb[s // 4][:, s % 4, :]
-            if s in (0, 1, 6):
-                h1[s] = tile([P, S], F32, "h1_%d" % s, {0: "h6", 1: "h0", 6: "y_half1"}[s])[:]
-                nc.vector.tensor_tensor(h1[s], s_acc[s][:], b, ADD)
-            elif s == 7:
-                h1[s] = tile([P, S], F32, "h1_%d" % s, "y_half1")[:]
-                nc.gpsimd.tensor_tensor(h1[s], s_sb[s][:], b, ADD)
+            h1[s] = tile([P, S], F32, "h1_%d" % s, ("h6", "h0", "h1", "h5", "h3", "h4", "h2", "y_half1")[s])[:]
+            if s in h1_acc:
+                nc.scalar.copy(out=h1[s], in_=h1_acc[s][:])
             else:
-                spare[s - 2] = tile([P, S + PJ], F32, "spare%d" % (s - 2), "page%d" % (s - 2))
-                h1[s] = spare[s - 2][:, :S]
-                nc.gpsimd.tensor_tensor(h1[s], s_sb[s][:], b, ADD)
+                nc.vector.tensor_tensor(h1[s], s_acc[s][:], b_sb[s // 4][:, s % 4, :], ADD)
 
         w4_codes = tile([P, 2 * N], U32, "w4_codes", "slotH")
         w4_sc = tile([P, 2 * N], U8, "w4_sc")
@@ -336,6 +340,8 @@ def tile_list_ballot_batch_slots_kernel(
             a, t = divmod(s, 4)
             x = x_home[s][:, j0 : j0 + width]
             th = tanh_x[:, j0 : j0 + width]
+            if s == SLICES - 1 and j0 >= PJ // 2:
+                x, th = tanh_x[:, j0 - PJ // 2 : j0 - PJ // 2 + width], x_home[s][:, j0 - PJ // 2 : j0 - PJ // 2 + width]
             nc.vector.tensor_copy(x, pages[s][:].indirect(idx5[:, j0 // 16 : (j0 + width) // 16]))
             nc.scalar.activation(th, x, ACT.Tanh)
             gain = gain2_sb[:, a, t : t + 1]
@@ -364,21 +370,17 @@ def tile_list_ballot_batch_slots_kernel(
                         start=(a == 0 and e == 0), stop=(a == 1 and e == 1),
                     )
 
-        add_b(0)
-        add_b(1)
+        for s in range(SLICES - 1):
+            add_b(s)
         last = SLICES - 1
         for s in range(SLICES):
-            if 3 <= s < last:
-                x_home[s] = spare[s - 3][:, S:]
-            elif s == last:
-                x_home[s] = tile([P, PJ], F32, "x_last", "page4")[:]
-            if s >= 6:
+            if s >= 3:
+                x_home[s] = tile([P, PJ], F32, "x_%d" % s, "page%d" % (s - 3))[:]
+            if s == last:
                 add_b(s)
             scatter1(s)
             if s < last:
                 fetch(s, 0, PJ)
-            if s + 2 < 6:
-                add_b(s + 2)
             if s < 2:
                 w4_pass(s)
             if s == 3:

from contextlib import ExitStack

import concourse.mybir as mybir
from concourse.masks import make_identity

K, T, T3, S, T2, PJ, H, N = 1024, 2048, 1024, 512, 2048, 1024, 1024, 512
FLOPS = 2 * S * K * H * 3 + 2 * PJ * H * N

F32 = mybir.dt.float32
BF16 = mybir.dt.bfloat16
I32 = mybir.dt.int32
U32 = mybir.dt.uint32
U16 = mybir.dt.uint16
U8 = mybir.dt.uint8
FP8X4 = mybir.dt.float8_e4m3fn_x4
FP4X4 = mybir.dt.float4_e2m1fn_x4
ACT = mybir.ActivationFunctionType
MULT = mybir.AluOpType.mult
ADD = mybir.AluOpType.add

P = 128
PASS = 512
SLICES = H // P
CH = 256
AL = 64


def tile_list_ballot_batch_slots_kernel(
    tc, tab_words, tab_scales, tab2_words, tab2_scales, offs, offs2, offs3, offs4, offs5,
    w1, w2_words, w2_scales, w3_words, w3_scales, w4, gain1, gain2, page0, wg1, wg2, out,
):
    nc = tc.nc
    with ExitStack() as ctx:
        lists = ctx.enter_context(tc.tile_pool(name="lists", bufs=1))
        sb = ctx.enter_context(tc.tile_pool(name="sb", bufs=1))
        ring = ctx.enter_context(tc.tile_pool(name="ring", bufs=3))
        psum = ctx.enter_context(tc.psum_pool(name="psum", bufs=1))

        def tile(shape, dtype, name, tag=None):
            return sb.tile(shape, dtype, name=name, tag=tag or name, align_bytes=AL)

        def bank(i, name):
            return psum.tile([P, 512], F32, name=name, tag="bank%d" % i)

        def load_list(src, name):
            dst = lists.tile(list(src.shape), U16, name=name)
            nc.sync.dma_start(dst[:], src)
            return dst

        def load_words(dst, words, a):
            nc.sync.dma_start(out=dst, in_=words[a].rearrange("p t i -> p (t i)").bitcast(I32))

        def zeroed(shape, name):
            dst = tile(shape, U8, name)
            nc.vector.memset(dst[:].bitcast(I32), 0)
            return dst

        def load_packed_scales(dst, scales):
            for q in range(4):
                nc.sync.dma_start(out=dst[32 * q : 32 * q + 8, :].bitcast(I32), in_=scales[:, 4 * q : 4 * q + 4, :].bitcast(I32))

        def load_wg_dealt(src, name, tag):
            dst = tile([P, 4, S], F32, name, tag)
            for q in (0, 2, 1, 3):
                nc.sync.dma_start(out=dst[32 * q : 32 * q + 32, :, :], in_=src.rearrange("(p t) s -> p t s", t=4))
            return dst

        def load_wg(src, name, spare):
            rows = ring.tile([P, S], F32, name=name + "_rows", tag="tanh_b")
            nc.sync.dma_start(out=rows[:], in_=src)
            turned = bank(0, name + "_turned")
            for c in range(4):
                nc.tensor.transpose(turned[:, c * P : (c + 1) * P], rows[:, c * P : (c + 1) * P], ident[:])
            spread = tile([P, 4, 4, 4, 32], F32, name + "_spread", spare)
            nc.scalar.copy(out=spread[:], in_=turned[:].rearrange("j (c q t) -> j c t q", c=4, t=4).unsqueeze(3).to_broadcast([P, 4, 4, 4, 32]))
            dst = tile([P, 4, S], F32, name)
            for t in range(4):
                back = bank(t, name + "_back%d" % t)
                for c in range(4):
                    nc.tensor.transpose(back[:, c * P : (c + 1) * P], spread[:, c, t, :, :].rearrange("j x q -> j (x q)"), ident[:])
                nc.scalar.copy(out=dst[:, t, :], in_=back[:])
            return dst

        def load_gain(src, name):
            dst = tile([P, 2, 4], F32, name)
            nc.sync.dma_start(out=dst[:], in_=src.rearrange("(a p t) -> p a t", a=2, t=4))
            return dst

        def load_page(s):
            a, t = divmod(s, 4)
            dst = tile([P, T2], F32, "page%d" % s)
            nc.sync.dma_start(out=dst[:], in_=page0[PASS * a : PASS * (a + 1), :].rearrange("(p t) c -> p t c", t=4)[:, t, :])
            return dst

        def load_rows(src, a, cols, name, tag):
            dst = tile([P, 4, 512], F32, name, tag)
            nc.sync.dma_start(out=dst[:], in_=src[PASS * a : PASS * (a + 1), cols].rearrange("(p j) c -> p j c", j=4))
            return dst

        def quantize(codes, scales, grouped):
            nc.vector.quantize_mx(out=codes.bitcast(FP8X4), scales=scales, in_=grouped)

        def interleave(copy, rows, width, name, tag=None):
            if tag:
                grouped = tile([P, 4 * width], BF16, name, tag)
            else:
                grouped = ring.tile([P, 4 * width], BF16, name=name, tag="grouped", align_bytes=AL)
            copy(out=grouped[:].rearrange("p (c i t) -> p c t i", i=4, t=4), in_=rows.rearrange("p t (c i) -> p c t i", i=4))
            return grouped

        ident = tile([P, P], F32, "ident")
        make_identity(nc, ident[:])

        tab2_sc = zeroed([P, T3], "tab2_sc")
        tab_sc = zeroed([P, T], "tab_sc")
        w3_sc_raw = zeroed([P, H], "w3_sc_raw")
        w2_sc_raw = zeroed([P, 2 * H], "w2_sc_raw")

        def gather_table(windows, scales, idx, name):
            codes = [tile([P, S], U32, "%s_%d" % (name, a)) for a in range(2)]
            for a in range(2):
                nc.vector.tensor_copy(codes[a][:], windows[a].bitcast(U32).indirect(idx[:]))
            plane = tile([P, S], U8, name + "_sc")
            nc.vector.tensor_copy(plane[:], scales[:].indirect(idx[:]))
            return codes, plane

        idx2 = load_list(offs2, "idx2")
        idx1 = load_list(offs, "idx1")
        idx4 = load_list(offs4, "idx4")
        idx3 = load_list(offs3, "idx3")

        w1_codes = {}
        w1_grouped = {}
        w1_sc = tile([P, 2 * H], U8, "w1_sc")
        b_sb = {}
        b_acc = {}
        t_codes = {}
        t_sc = tile([P, 2 * S], U8, "t_sc")

        def w1_chunk(a, b):
            raw = load_rows(w1, a, slice(512 * b, 512 * (b + 1)), "w1_raw%d%d" % (a, b), "slot" + "EFAB"[2 * b + a])
            grouped = ring.tile([P, 2048], BF16, name="w1_g%d%d" % (a, b), tag="grouped", align_bytes=AL)
            cast = nc.vector.tensor_copy if (a, b) == (1, 0) else nc.scalar.copy
            cast(out=grouped[:].rearrange("p (t m j) -> p m j t", t=4, j=4), in_=raw[:].rearrange("p j (m t) -> p m j t", t=4))
            w1_grouped[a, b] = grouped

        def quantize_w1(a, b):
            grouped = w1_grouped[a, b]
            cols = slice(a * H + 512 * b, a * H + 512 * (b + 1))
            w1_codes[a, b] = tile([P, 512], U32, "w1_codes%d%d" % (a, b), "h%d" % (3, 4)[a] if b else "slot" + "DH"[a])
            quantize(w1_codes[a, b][:], w1_sc[:, cols], grouped[:])

        def first_stage(b):
            accs = []
            t_rows = tile([P, 4, S], BF16, "t_rows%d" % b)
            for t in range(4):
                s = 4 * b + t
                acc = bank(s, "b_acc%d" % s)
                for a in range(2):
                    cols = slice(a * H + s * P, a * H + (s + 1) * P)
                    nc.tensor.matmul_mx(
                        out=acc[:], lhsT=w1_codes[a, b][:, t * P : (t + 1) * P].bitcast(FP8X4), lhsT_scale=w1_sc[:, cols],
                        rhs=v[a][:].bitcast(FP8X4), rhs_scale=v_sc[4 * a : P, :], start=(a == 0), stop=(a == 1),
                    )
                th = ring.tile([P, S], F32, name="tanh_b%d" % s, tag="tanh_b")
                nc.scalar.activation(th[:], acc[:], ACT.Tanh)
                nc.scalar.activation(t_rows[:, t, :], th[:], ACT.Copy, scale=gain1_sb[:, b, t : t + 1])
                accs.append(acc)
            grouped = interleave(nc.scalar.copy, t_rows[:], S, "t_g%d" % b)
            t_grouped[b] = grouped
            b_acc[b] = accs

        def keep_b(b):
            b_sb[b] = tile([P, 4, S], F32, "b_sb%d" % b, ("slotB", "t_rows1")[b])
            for t in range(4):
                nc.scalar.copy(out=b_sb[b][:, t, :], in_=b_acc[b][t][:])

        def quantize_t(b):
            t_codes[b] = tile([P, S], U32, "t_codes%d" % b, "h%d" % (2, 7)[b])
            quantize(t_codes[b][:], t_sc[:, b * S : (b + 1) * S], t_grouped[b][:])

        h2 = {}
        t_grouped = {}

        def square_stage(b):
            for s in range(4 * b, 4 * b + 4):
                acc = bank((s + 4) % SLICES, "h2_acc%d" % s)
                for a in range(2):
                    nc.tensor.matmul_mx(
                        out=acc[:], lhsT=w3_d[:, a * H + s * P : a * H + (s + 1) * P].bitcast(FP8X4),
                        lhsT_scale=w3_sc[4 * a : P, s * P : (s + 1) * P],
                        rhs=v2[a][:].bitcast(FP8X4), rhs_scale=v2_sc[4 * a : P, :], start=(a == 0), stop=(a == 1),
                    )
                h2[s] = tile([P, S], F32, "h2_%d" % s, "h%d" % s)
                nc.scalar.activation(h2[s][:], acc[:], ACT.Square)

        pages = []

        def next_page():
            s = len(pages)
            pages.append(load_page(s))
            nc.vector.tensor_tensor(pages[s][:].indirect(idx4[:]), h2[s][:], wg2_sb[:, s % 4, :], MULT)

        tab2_w = tile([P, 2 * T3], I32, "tab2_w", "slotA")
        for a in range(2):
            load_words(tab2_w[:, a * T3 : (a + 1) * T3], tab2_words, a)
        load_packed_scales(tab2_sc, tab2_scales)
        v2, v2_sc = gather_table([tab2_w[:, a * T3 : (a + 1) * T3] for a in range(2)], tab2_sc, idx2, "v2")

        wg2_sb = load_wg(wg2, "wg2_sb", "page6")
        w3_raw = tile([P, 2 * H], I32, "w3_raw", "slotB")
        for a in range(2):
            load_words(w3_raw[:, a * H : (a + 1) * H], w3_words, a)
        load_packed_scales(w3_sc_raw, w3_scales)
        w3_d = tile([P, 2 * H], I32, "w3_d", "slotG")
        for a in range(2):
            cols = slice(a * H, (a + 1) * H)
            nc.vector.tensor_copy(
                out=w3_d[:, cols].rearrange("p (b t u i) -> p b u t i", b=2, t=4, i=4),
                in_=w3_raw[:, cols].rearrange("p (b u i t) -> p b u t i", b=2, t=4, i=4),
            )
        w3_sc = tile([P, H], U8, "w3_sc")
        nc.vector.tensor_copy(
            out=w3_sc[:].rearrange("p (b t q) -> p b t q", b=2, t=4),
            in_=w3_sc_raw[:].rearrange("p (b q t) -> p b t q", b=2, t=4),
        )

        square_stage(0)
        square_stage(1)
        w2_raw = tile([P, H], I32, "w2_raw", "slotH")
        nc.sync.dma_start(out=w2_raw[:].rearrange("p (a c) -> p a c", a=2), in_=w2_words.rearrange("a p c -> p a c").bitcast(I32))
        for q in range(4):
            nc.sync.dma_start(
                out=w2_sc_raw[32 * q : 32 * q + 4, :].bitcast(I32).rearrange("r (a c) -> r a c", a=2),
                in_=w2_scales[:, 4 * q : 4 * q + 4, :].rearrange("a r c -> r a c").bitcast(I32),
            )
        w2_d = tile([P, 4 * H], U8, "w2_d")
        nc.vector.tensor_copy(
            out=w2_d[:].bitcast(U16).rearrange("p (g t q) -> p g t q", g=4, t=4),
            in_=w2_raw[:].bitcast(U16).rearrange("p (g q t) -> p g t q", g=4, t=4),
        )
        w2_sc = tile([P, 2 * H], U8, "w2_sc")
        nc.vector.tensor_copy(
            out=w2_sc[:].rearrange("p (g t q) -> p g t q", g=4, t=4),
            in_=w2_sc_raw[:].rearrange("p (g q t) -> p g t q", g=4, t=4),
        )

        next_page()
        w1_chunk(0, 0)
        tab_w = [tile([P, T], I32, "tab_w%d" % a, "slot" + "CD"[a]) for a in range(2)]
        for a in range(2):
            load_words(tab_w[a][:], tab_words, a)
        load_packed_scales(tab_sc, tab_scales)
        v, v_sc = gather_table([w[:] for w in tab_w], tab_sc, idx1, "v")

        quantize_w1(0, 0)
        gain1_sb = load_gain(gain1, "gain1_sb")
        w1_chunk(1, 0)
        next_page()
        quantize_w1(1, 0)
        first_stage(0)
        next_page()
        w1_chunk(0, 1)
        next_page()
        w1_chunk(1, 1)
        quantize_t(0)
        quantize_w1(0, 1)
        next_page()
        quantize_w1(1, 1)
        keep_b(0)
        first_stage(1)
        keep_b(1)
        next_page()
        next_page()
        next_page()
        quantize_t(1)
        wg1_sb = load_wg_dealt(wg1, "wg1_sb", "slotG")
        idx5 = load_list(offs5, "idx5")
        gain2_sb = load_gain(gain2, "gain2_sb")

        s_acc = []
        for s in range(SLICES):
            acc = bank(s, "s_acc%d" % s)
            for a in range(2):
                c0 = a * H + s * P
                nc.tensor.matmul_mx(
                    out=acc[:], lhsT=w2_d[:, 2 * c0 : 2 * (c0 + P)].bitcast(FP4X4), lhsT_scale=w2_sc[:, c0 : c0 + P],
                    rhs=t_codes[a][:].bitcast(FP8X4), rhs_scale=t_sc[:, a * S : (a + 1) * S],
                    start=(a == 0), stop=(a == 1),
                )
            s_acc.append(acc)

        def turn(dst, parts):
            for c in range(4):
                cols = slice(c * P, (c + 1) * P)
                for i, part in enumerate(parts):
                    nc.tensor.matmul(dst[:, cols], part[:, cols], ident[:], start=(i == 0), stop=(i == len(parts) - 1), is_transpose=True)

        h1_acc = {}
        for s in (2, 3, 4, 5, 6):
            s_sb = ring.tile([P, S], F32, name="s_sb%d" % s, tag="tanh_b")
            nc.scalar.copy(out=s_sb[:], in_=s_acc[s][:])
            turned = bank(s, "h1_turned%d" % s)
            turn(turned, [b_sb[s // 4][:, s % 4, :], s_sb])
            turned_sb = ring.tile([P, S], F32, name="h1_turned_sb%d" % s, tag="tanh_b")
            nc.scalar.copy(out=turned_sb[:], in_=turned[:])
            h1_acc[s] = bank(s, "h1_acc%d" % s)
            turn(h1_acc[s], [turned_sb])

        h1 = {}

        def add_b(s):
            h1[s] = tile([P, S], F32, "h1_%d" % s, ("h6", "h0", "h1", "h5", "h3", "h4", "h2", "y_half1")[s])[:]
            if s in h1_acc:
                nc.scalar.copy(out=h1[s], in_=h1_acc[s][:])
            else:
                nc.vector.tensor_tensor(h1[s], s_acc[s][:], b_sb[s // 4][:, s % 4, :], ADD)

        w4_codes = tile([P, 2 * N], U32, "w4_codes", "slotH")
        w4_sc = tile([P, 2 * N], U8, "w4_sc")

        def w4_pass(a):
            raw = load_rows(w4, a, slice(0, N), "w4_raw%d" % a, "slot" + "CD"[a])
            grouped = interleave(nc.scalar.copy, raw[:], N, "w4_g%d" % a)
            quantize(w4_codes[:, a * N : (a + 1) * N], w4_sc[:, a * N : (a + 1) * N], grouped[:])

        x_sb = tile([P, 2, PJ], F32, "x_sb", "slotE")
        x_more = tile([P, 2, PJ], F32, "x_more", "slotF")
        tanh_x = x_more[:, 0, :]
        x_home = {0: x_sb[:, 0, :], 1: x_sb[:, 1, :], 2: x_more[:, 1, :]}
        y_rows = tile([P, 4, PJ], BF16, "y_rows", "slotA")
        y_woven = tile([P, PJ, 4], BF16, "y_woven", "slotB")
        y_codes = tile([P, 2 * PJ], U32, "y_codes", "slotI")
        y_sc = tile([P, 2 * PJ], U8, "y_sc")

        def scatter1(s):
            nc.vector.tensor_tensor(pages[s][:].indirect(idx3[:]), h1[s], wg1_sb[:, s % 4, :], MULT)

        def fetch(s, j0, width):
            a, t = divmod(s, 4)
            x = x_home[s][:, j0 : j0 + width]
            th = tanh_x[:, j0 : j0 + width]
            if s == SLICES - 1 and j0 >= PJ // 2:
                x, th = tanh_x[:, j0 - PJ // 2 : j0 - PJ // 2 + width], x_home[s][:, j0 - PJ // 2 : j0 - PJ // 2 + width]
            nc.vector.tensor_copy(x, pages[s][:].indirect(idx5[:, j0 // 16 : (j0 + width) // 16]))
            nc.scalar.activation(th, x, ACT.Tanh)
            gain = gain2_sb[:, a, t : t + 1]
            if s == SLICES - 1:
                nc.vector.tensor_scalar(y_woven[:, j0 : j0 + width, t], th, gain, None, MULT)
            else:
                y = y_rows[:, t, j0 : j0 + width] if a == 0 else y_woven[:, j0 : j0 + width, t]
                nc.scalar.activation(y, th, ACT.Copy, scale=gain)

        def quantize_y(a, j0, width, grouped):
            cols = slice(a * PJ + j0, a * PJ + j0 + width)
            quantize(y_codes[:, cols], y_sc[:, cols], grouped)

        out_acc = {}

        def out_pass(a, q):
            cols = slice(a * PJ + q * CH, a * PJ + (q + 1) * CH)
            for h in range(2):
                if a == 0:
                    out_acc[q, h] = bank(2 * q + h, "out_acc%d%d" % (q, h))
                for e in range(2):
                    wc = slice(a * N + (2 * h + e) * P, a * N + (2 * h + e + 1) * P)
                    nc.tensor.matmul_mx(
                        out=out_acc[q, h][:, e * CH : (e + 1) * CH], lhsT=w4_codes[:, wc].bitcast(FP8X4), lhsT_scale=w4_sc[:, wc],
                        rhs=y_codes[:, cols].bitcast(FP8X4), rhs_scale=y_sc[:, cols],
                        start=(a == 0 and e == 0), stop=(a == 1 and e == 1),
                    )

        for s in range(SLICES - 1):
            add_b(s)
        last = SLICES - 1
        for s in range(SLICES):
            if s >= 3:
                x_home[s] = tile([P, PJ], F32, "x_%d" % s, "page%d" % (s - 3))[:]
            if s == last:
                add_b(s)
            scatter1(s)
            if s < last:
                fetch(s, 0, PJ)
            if s < 2:
                w4_pass(s)
            if s == 3:
                for j0 in (0, 512):
                    quantize_y(0, j0, 512, interleave(nc.scalar.copy, y_rows[:, :, j0 : j0 + 512], 512, "y_g%d" % j0, "y_half%d" % (j0 // 512))[:])
        for q in range(PJ // CH):
            out_pass(0, q)
        staged = [tile([P, 4, 2 * CH], F32, "staged%d" % h, "slot" + "CD"[h]) for h in range(2)]
        out_view = out.rearrange("(c p) j -> p c j", p=P)
        for q in range(PJ // CH):
            fetch(last, q * CH, CH)
        for q in range(PJ // CH):
            quantize_y(1, q * CH, CH, y_woven[:, q * CH : (q + 1) * CH, :].rearrange("p j t -> p (j t)"))
            out_pass(1, q)
            for h in range(2):
                copy = nc.scalar.copy if (h == 0 or q < 2) else nc.vector.tensor_copy
                copy(out=staged[h][:, q, :], in_=out_acc[q, h][:])
                nc.sync.dma_start(
                    out=out_view[:, 2 * h : 2 * h + 2, q * CH : (q + 1) * CH],
                    in_=staged[h][:, q, :].rearrange("p (e j) -> p e j", e=2),
                )
